import numpy as np
import ml_dtypes


def mxq(x, axis, fmt="e4m3"):
    dtype, down = {"e4m3": (ml_dtypes.float8_e4m3fn, 7), "e5m2": (ml_dtypes.float8_e5m2, 14)}[fmt]
    v = np.moveaxis(np.asarray(x, np.float32).astype(ml_dtypes.bfloat16).astype(np.float64), axis, -1)
    blocks = v.reshape(v.shape[:-1] + (-1, 32))
    amax = np.abs(blocks).max(-1, keepdims=True)
    byte = np.maximum(np.where(amax > 0, np.frexp(amax)[1] - 1 + 127, 0) - down, 1)
    scale = np.exp2(byte - 127.0)
    codes = (blocks / scale).astype(np.float32).astype(dtype).astype(np.float64)
    return np.moveaxis((codes * scale).reshape(v.shape), -1, axis)


WIDE = False


def mx_kscale(k):
    if not WIDE:
        return np.ones(k)
    levels = np.array([30, -30])
    if k % 512:
        return np.exp2(np.random.permutation(np.resize(levels, k // 32))).repeat(32)
    a = np.empty((k // 512, 16))
    for p in range(k // 512):
        a[p, :8] = np.random.permutation(np.resize(levels, 8))
        for g in range(8):
            far = levels[np.abs(levels - a[p, g]) >= 10]
            a[p, g + 8] = far[np.random.randint(len(far))]
    return np.exp2(a.ravel()).repeat(32)


def f64(x):
    return np.asarray(x).astype(np.float64)


def striped(idx):
    return np.tile(np.asarray(idx).reshape(-1, 16).T, (8, 1)).astype(np.uint16)


def unstriped(offs):
    return offs[:16].T.reshape(-1).astype(np.int64)


E2M1 = np.array([0.0, 0.5, 1.0, 1.5, 2.0, 3.0, 4.0, 6.0, -0.0, -0.5, -1.0, -1.5, -2.0, -3.0, -4.0, -6.0])


def pack_weight(w, fmt):
    k, n = w.shape
    w = f64(np.asarray(w, np.float32).astype(ml_dtypes.bfloat16)).reshape(k // 32, 32, n)
    amax = np.abs(w).max(1)
    if fmt == "e4m3":
        byte = np.frexp(amax)[1] - 1 + 127 - 7
    else:
        mant, ex = np.frexp(amax / 6.0)
        byte = np.where(mant > 0.5, ex, ex - 1) + 127
    byte = np.clip(np.where(amax > 0, byte, 1), 1, 254)
    scaled = (w * np.exp2(127.0 - byte)[:, None, :]).reshape(k, n).astype(np.float32)
    by_word = np.ascontiguousarray(scaled.reshape(k // 512, 128, 4, n).transpose(0, 1, 3, 2))
    if fmt == "e4m3":
        words = by_word.astype(ml_dtypes.float8_e4m3fn).view(np.uint8)
    else:
        c = by_word.astype(ml_dtypes.float4_e2m1fn).view(np.uint8) & 0xF
        words = (c[..., 0::2] | (c[..., 1::2] << 4)).reshape(k // 512, 128, 2 * n)
    return np.ascontiguousarray(words), np.ascontiguousarray(byte.astype(np.uint8).reshape(k // 512, 16, n))


def unpack_weight(words, scales, fmt):
    g, _, n = scales.shape
    words = np.ascontiguousarray(words).reshape(g, 128, n, -1)
    if fmt == "e4m3":
        vals = words.view(ml_dtypes.float8_e4m3fn).astype(np.float64)
    else:
        nib = np.empty((g, 128, n, 4), np.uint8)
        nib[..., 0::2] = words & 0xF
        nib[..., 1::2] = words >> 4
        vals = E2M1[nib]
    vals = vals * np.repeat(np.exp2(scales.astype(np.float64) - 127.0), 8, axis=1)[..., None]
    return vals.transpose(0, 1, 3, 2).reshape(g * 512, n)


def sigmoid(v):
    return 1.0 / (1.0 + np.exp(-v))


K, T, J, R, F, Z, N = 512, 512, 256, 512, 512, 1024, 256


def setup_inputs():
    n = np.random.standard_normal
    idx = np.random.permutation(T)[:J]
    idx2 = np.random.permutation(Z)[:J]
    fk = mx_kscale(K)
    fr = mx_kscale(R)
    ff = mx_kscale(F)
    wp = pack_weight(n((K, R)) * 1 / np.sqrt(K) * fk[:, None] * fr, "e2m1")
    w2p = pack_weight(n((F, R)) * 1 / np.sqrt(F) * ff[:, None] * fr, "e2m1")
    wbp = pack_weight(n((R, N)) * 1 / np.sqrt(R) / fr[:, None], "e2m1")
    return {
        "xf": (n((K, T))).astype(np.float32),
        "fk": (np.random.uniform(0.5, 2.0, (K, 1)) / fk[:, None]).astype(np.float32),
        "w_words": wp[0],
        "w_scales": wp[1],
        "xo": (n((F, Z))).astype(np.float32),
        "fl": (np.random.uniform(0.5, 2.0, (F, 1)) / ff[:, None]).astype(np.float32),
        "so": (n((F, J))).astype(np.float32),
        "w2_words": w2p[0],
        "w2_scales": w2p[1],
        "wb_words": wbp[0],
        "wb_scales": wbp[1],
        "rs": (n((N, J))).astype(np.float32),
        "gm": (np.random.uniform(0.5, 2.0, (N, 1))).astype(np.float32),
        "offs": striped(idx),
        "offs2": striped(idx2),
    }


def reference(xf, fk, w_words, w_scales, xo, fl, so, w2_words, w2_scales, wb_words, wb_scales, rs, gm, offs, offs2):
    idx = unstriped(offs)
    idx2 = unstriped(offs2)
    wu = unpack_weight(w_words, w_scales, "e2m1")
    w2u = unpack_weight(w2_words, w2_scales, "e2m1")
    wbu = unpack_weight(wb_words, wb_scales, "e2m1")
    xg = f64(xf)[:, idx]
    x1 = np.pad(xg, ((0, 0), (1, 0)))[:, :J]
    u = (xg - 0.6 * x1) * f64(fk)
    u2 = f64(xo)[:, idx2] * sigmoid(f64(so)) * f64(fl)
    uq = mxq(u, 0, "e4m3")
    u2q = mxq(u2, 0, "e5m2")
    a = wu.T @ uq + w2u.T @ u2q
    ha = np.maximum(a, 0.0)
    h1 = np.pad(ha, ((0, 0), (2, 0)))[:, :J]
    hid = ha - 0.5 * h1
    hidq = mxq(hid, 0, "e5m2")
    p = wbu.T @ hidq
    y = f64(gm) * p + f64(rs)
    return y

@@ -1,0 +1,235 @@
+from contextlib import ExitStack
+
+import concourse.mybir as mybir
+
+K, T, J, R, F, Z, N = 512, 512, 256, 512, 512, 1024, 256
+FLOPS = 2 * J * (K * R + F * R + R * N)
+
+F32 = mybir.dt.float32
+BF16 = mybir.dt.bfloat16
+I32 = mybir.dt.int32
+U32 = mybir.dt.uint32
+U16 = mybir.dt.uint16
+U8 = mybir.dt.uint8
+E4M3 = mybir.dt.float8_e4m3fn_x4
+E5M2 = mybir.dt.float8_e5m2_x4
+E2M1 = mybir.dt.float4_e2m1fn_x4
+ALU = mybir.AluOpType
+ACT = mybir.ActivationFunctionType
+
+P = 128
+PACK = 4
+HALF = J // 2
+PAD = 4
+
+
+def tile_list_sum_steps_gated_lagged_residual_kernel(
+    tc, xf, fk, w_words, w_scales, xo, fl, so, w2_words, w2_scales, wb_words, wb_scales, rs, gm, offs, offs2, out
+):
+    nc = tc.nc
+    with ExitStack() as ctx:
+        pool = ctx.enter_context(tc.tile_pool(name="keep", bufs=1))
+        psum = ctx.enter_context(tc.psum_pool(name="psum", bufs=1))
+
+        raw_scales = pool.tile([P, 2 * R + N], U8, name="raw_scales")
+        nc.gpsimd.memset(raw_scales[:].bitcast(I32), 0)
+        offs_sb = pool.tile([P, J // 16], U16, name="offs_sb")
+        nc.sync.dma_start(offs_sb[:], offs)
+        xf_rows = xf.rearrange("(p t) c -> p t c", t=PACK)
+        xf_sb = [pool.tile([P, 2, T], F32, name=f"xf_sb{u}") for u in range(2)]
+        nc.sync.dma_start(xf_sb[0][:], xf_rows[:, 0:2, :])
+        for c0, scales in ((0, w_scales), (R, w2_scales), (2 * R, wb_scales)):
+            width = scales.shape[2]
+            nc.sync.dma_start(raw_scales[0:16, c0 : c0 + width].bitcast(I32), scales[0].bitcast(I32))
+        fk_sb = pool.tile([P, PACK], F32, name="fk_sb")
+        nc.sync.dma_start(fk_sb[:], fk.rearrange("(p t) o -> p (t o)", t=PACK))
+        so_sb = pool.tile([P, PACK, J], F32, name="so_sb")
+        nc.sync.dma_start(so_sb[:], so.rearrange("(p t) j -> p t j", t=PACK))
+        fl_sb = pool.tile([P, PACK], F32, name="fl_sb")
+        nc.sync.dma_start(fl_sb[:], fl.rearrange("(p t) o -> p (t o)", t=PACK))
+        nc.sync.dma_start(xf_sb[1][:], xf_rows[:, 2:4, :])
+        raw_words = []
+        for g, words in enumerate((w_words, w2_words)):
+            raw = pool.tile([P, 2 * R], U8, name=f"raw_words{g}")
+            nc.sync.dma_start(raw[:].bitcast(I32), words[0].bitcast(I32))
+            raw_words.append(raw)
+        offs2_sb = pool.tile([P, J // 16], U16, name="offs2_sb")
+        nc.sync.dma_start(offs2_sb[:], offs2)
+        xo_rows = xo.rearrange("(p t) c -> p t c", t=PACK)
+        xo_sb = []
+        for t in range(PACK):
+            plane = pool.tile([P, Z], F32, name=f"xo_sb{t}")
+            nc.sync.dma_start(plane[:], xo_rows[:, t, :])
+            xo_sb.append(plane)
+        wb_sb = pool.tile([P, 2 * N], U8, name="wb_sb", align_bytes=64)
+        nc.sync.dma_start(wb_sb[:].bitcast(I32), wb_words[0].bitcast(I32))
+        gm_sb = pool.tile([P, 2, 1], F32, name="gm_sb")
+        with nc.allow_non_contiguous_dma(reason="one factor a partition and output tile"):
+            nc.sync.dma_start(gm_sb[:], gm.rearrange("(h p) o -> p h o", p=P))
+        rs_sb = pool.tile([P, 2, J], F32, name="rs_sb")
+        nc.sync.dma_start(rs_sb[:], rs.rearrange("(h p) j -> p h j", p=P))
+
+
+        w_sc = pool.tile([P, 2 * R + N], U8, name="w_sc", align_bytes=64)
+        nc.vector.tensor_copy(
+            w_sc[:, 0 : 2 * R].rearrange("p (g t m) -> p g t m", g=2, t=PACK),
+            raw_scales[:, 0 : 2 * R].rearrange("p (g m t) -> p g t m", g=2, t=PACK),
+        )
+        nc.vector.tensor_copy(w_sc[:, 2 * R :].bitcast(I32), raw_scales[:, 2 * R :].bitcast(I32))
+        for q in range(1, 4):
+            nc.gpsimd.dma_start(w_sc[32 * q : 32 * q + 4, :].bitcast(I32), w_sc[4 * q : 4 * q + 4, :].bitcast(I32))
+
+        picked = []
+        for u in range(2):
+            pair = pool.tile([P, 2, PAD + J], F32, name=f"picked{u}")
+            nc.vector.memset(pair[:, :, PAD - 1 : PAD], 0.0)
+            picked.append(pair)
+        ha = pool.tile([P, (2 + J) * PACK], F32, name="ha")
+        nc.vector.memset(ha[:, 0 : 2 * PACK], 0.0)
+
+        steps = pool.tile([P, PACK, J], F32, name="steps")
+        u = pool.tile([P, PACK, J], F32, name="u")
+        for t in range(2):
+            nc.vector.tensor_copy(picked[0][:, t, PAD:], xf_sb[0][:, t, :].indirect(offs_sb[:]))
+        nc.vector.scalar_tensor_tensor(
+            steps[:, 0:2, :], picked[0][:, :, PAD - 1 : PAD - 1 + J], -0.6, picked[0][:, :, PAD:], ALU.mult, ALU.add
+        )
+        for t in range(2):
+            nc.vector.tensor_scalar(u[:, t, :], steps[:, t, :], fk_sb[:, t : t + 1], None, ALU.mult)
+        sig = pool.tile([P, PACK, J], F32, name="sig")
+        nc.scalar.activation(sig[:], so_sb[:], ACT.Sigmoid)
+        nc.vector.tensor_copy(picked[1][:, 0, PAD:], xf_sb[1][:, 0, :].indirect(offs_sb[:]))
+        nc.scalar.activation(picked[1][:, 1, PAD:], xf_sb[1][:, 1, :].indirect(offs_sb[:]), ACT.Copy)
+        nc.vector.scalar_tensor_tensor(
+            steps[:, 2:4, :], picked[1][:, :, PAD - 1 : PAD - 1 + J], -0.6, picked[1][:, :, PAD:], ALU.mult, ALU.add
+        )
+        gate = pool.tile([P, PACK, J], F32, name="gate")
+        for t in range(PACK):
+            nc.scalar.activation(gate[:, t, :], sig[:, t, :], ACT.Copy, scale=fl_sb[:, t : t + 1])
+        w_sb = []
+        for g in range(2):
+            dealt = pool.tile([P, 2 * R], U8, name=f"w_sb{g}", align_bytes=64)
+            nc.vector.tensor_copy(
+                dealt[:].bitcast(U16).rearrange("p (t m) -> p t m", t=PACK),
+                raw_words[g][:].bitcast(U16).rearrange("p (m t) -> p t m", t=PACK),
+            )
+            w_sb.append(dealt)
+        for t in range(2, PACK):
+            nc.scalar.activation(u[:, t, :], steps[:, t, :], ACT.Copy, scale=fk_sb[:, t : t + 1])
+        u_bf = pool.tile([P, J * PACK], BF16, name="u_bf", align_bytes=64)
+        nc.scalar.copy(
+            u_bf[:].rearrange("p (c i t) -> p c t i", i=4, t=PACK), u[:].rearrange("p t (c i) -> p c t i", i=4)
+        )
+
+        u2 = pool.tile([P, PACK, J], F32, name="u2")
+        for t in range(2):
+            nc.vector.tensor_tensor(u2[:, t, :], xo_sb[t][:].indirect(offs2_sb[:]), gate[:, t, :], ALU.mult)
+
+        u_codes = pool.tile([P, J], U32, name="u_codes", align_bytes=64)
+        u_sc = pool.tile([P, J], U8, name="u_sc", align_bytes=64)
+        nc.vector.quantize_mx(out=u_codes[:].bitcast(E4M3), scales=u_sc[:], in_=u_bf[:])
+        acc = [psum.tile([P, PACK, HALF], F32, name=f"acc{s}") for s in range(2)]
+        for s in range(2):
+            cols = slice(s * HALF, (s + 1) * HALF)
+            for t in range(PACK):
+                nc.tensor.matmul_mx(
+                    acc[s][:, t, :],
+                    lhsT=w_sb[0][:, 2 * P * t : 2 * P * (t + 1)].bitcast(E2M1),
+                    lhsT_scale=w_sc[:, P * t : P * (t + 1)],
+                    rhs=u_codes[:, cols].bitcast(E4M3),
+                    rhs_scale=u_sc[:, cols],
+                    start=(t == 0),
+                    stop=False,
+                )
+
+        nc.vector.tensor_tensor(u2[:, 2, :], xo_sb[2][:].indirect(offs2_sb[:]), gate[:, 2, :], ALU.mult)
+
+        u2_bf = [pool.tile([P, HALF * PACK], BF16, name=f"u2_bf{s}", align_bytes=64) for s in range(2)]
+        u2_codes = [pool.tile([P, HALF], U32, name=f"u2_codes{s}", align_bytes=64) for s in range(2)]
+        u2_sc = [pool.tile([P, HALF], U8, name=f"u2_sc{s}", align_bytes=64) for s in range(2)]
+        hid_bf = [pool.tile([P, HALF * PACK], BF16, name=f"hid_bf{s}", align_bytes=64) for s in range(2)]
+        hid_codes = [pool.tile([P, HALF], U32, name=f"hid_codes{s}", align_bytes=64) for s in range(2)]
+        hid_sc = [pool.tile([P, HALF], U8, name=f"hid_sc{s}", align_bytes=64) for s in range(2)]
+        prod = [psum.tile([P, 2, HALF], F32, name=f"prod{s}") for s in range(2)]
+        res = [pool.tile([P, 2, HALF], F32, name=f"res{s}") for s in range(2)]
+        out_rows = out.rearrange("(h p) j -> p h j", p=P)
+
+        def gather_last(s):
+            cols = slice(s * HALF, (s + 1) * HALF)
+            lst = offs2_sb[:, s * HALF // 16 : (s + 1) * HALF // 16]
+            nc.vector.tensor_tensor(u2[:, 3, cols], xo_sb[3][:].indirect(lst), gate[:, 3, cols], ALU.mult)
+
+        def weave(s, copy):
+            cols = slice(s * HALF, (s + 1) * HALF)
+            copy(
+                u2_bf[s][:].rearrange("p (c i t) -> p c t i", i=4, t=PACK),
+                u2[:, :, cols].rearrange("p t (c i) -> p c t i", i=4),
+            )
+
+        def first_stage(s):
+            nc.vector.quantize_mx(out=u2_codes[s][:].bitcast(E5M2), scales=u2_sc[s][:], in_=u2_bf[s][:])
+            for t in range(PACK):
+                nc.tensor.matmul_mx(
+                    acc[s][:, t, :],
+                    lhsT=w_sb[1][:, 2 * P * t : 2 * P * (t + 1)].bitcast(E2M1),
+                    lhsT_scale=w_sc[:, R + P * t : R + P * (t + 1)],
+                    rhs=u2_codes[s][:].bitcast(E5M2),
+                    rhs_scale=u2_sc[s][:],
+                    start=False,
+                    stop=(t == PACK - 1),
+                )
+
+        QW = HALF // 2
+
+        def hidden(s):
+            for q in range(2):
+                j0 = s * HALF + q * QW
+                nc.scalar.activation(
+                    ha[:, (2 + j0) * PACK : (2 + j0 + QW) * PACK].rearrange("p (j t) -> p j t", t=PACK),
+                    acc[s][:, :, q * QW : (q + 1) * QW].rearrange("p t j -> p j t"),
+                    ACT.Relu,
+                )
+            for q in range(2):
+                j0 = s * HALF + q * QW
+                nc.vector.scalar_tensor_tensor(
+                    hid_bf[s][:, q * QW * PACK : (q + 1) * QW * PACK],
+                    ha[:, j0 * PACK : (j0 + QW) * PACK],
+                    -0.5,
+                    ha[:, (2 + j0) * PACK : (2 + j0 + QW) * PACK],
+                    ALU.mult,
+                    ALU.add,
+                )
+
+        def second_stage(s):
+            nc.vector.quantize_mx(out=hid_codes[s][:].bitcast(E5M2), scales=hid_sc[s][:], in_=hid_bf[s][:])
+            for h in range(2):
+                nc.tensor.matmul_mx(
+                    prod[s][:, h, :],
+                    lhsT=wb_sb[:, 2 * P * h : 2 * P * (h + 1)].bitcast(E2M1),
+                    lhsT_scale=w_sc[:, 2 * R + P * h : 2 * R + P * (h + 1)],
+                    rhs=hid_codes[s][:].bitcast(E5M2),
+                    rhs_scale=hid_sc[s][:],
+                    start=True,
+                    stop=True,
+                )
+
+        def finish(s):
+            cols = slice(s * HALF, (s + 1) * HALF)
+            for h in range(2):
+                nc.vector.scalar_tensor_tensor(
+                    res[s][:, h, :], prod[s][:, h, :], gm_sb[:, h, :], rs_sb[:, h, cols], ALU.mult, ALU.add
+                )
+            nc.sync.dma_start(out_rows[:, :, cols], res[s][:])
+
+        gather_last(0)
+        gather_last(1)
+        weave(0, nc.vector.tensor_copy)
+        weave(1, nc.scalar.copy)
+        first_stage(0)
+        first_stage(1)
+        hidden(0)
+        second_stage(0)
+        hidden(1)
+        finish(0)
+        second_stage(1)
+        finish(1)

@@ -21,6 +21,7 @@ P = 128
 PACK = 4
 HALF = J // 2
 PAD = 4
+LEAD = 64
 
 
 def tile_list_sum_steps_gated_lagged_residual_kernel(
@@ -31,51 +32,57 @@ def tile_list_sum_steps_gated_lagged_residual_kernel(
         pool = ctx.enter_context(tc.tile_pool(name="keep", bufs=1))
         psum = ctx.enter_context(tc.psum_pool(name="psum", bufs=1))
 
-        raw_scales = pool.tile([P, 2 * R + N], U8, name="raw_scales")
+        raw_scales = pool.tile([P, 2 * R], U8, name="raw_scales")
         nc.gpsimd.memset(raw_scales[:].bitcast(I32), 0)
+        for g, scales in enumerate((w_scales, w2_scales)):
+            nc.sync.dma_start(raw_scales[0:16, g * R : (g + 1) * R].bitcast(I32), scales[0].bitcast(I32))
+        so_rows = so.rearrange("(p t) j -> p (t j)", t=PACK)
+        so_first = pool.tile([P, LEAD], F32, name="so_first")
+        nc.sync.dma_start(so_first[:], so_rows[:, 0:LEAD])
+        xf_rows = xf.rearrange("(p t) c -> p t c", t=PACK)
+        xf_sb = [pool.tile([P, T], F32, name=f"xf_sb{t}") for t in range(2)]
+        nc.sync.dma_start(xf_sb[0][:], xf_rows[:, 0, :])
         offs_sb = pool.tile([P, J // 16], U16, name="offs_sb")
         nc.sync.dma_start(offs_sb[:], offs)
-        xf_rows = xf.rearrange("(p t) c -> p t c", t=PACK)
-        xf_sb = [pool.tile([P, 2, T], F32, name=f"xf_sb{u}") for u in range(2)]
-        nc.sync.dma_start(xf_sb[0][:], xf_rows[:, 0:2, :])
-        for c0, scales in ((0, w_scales), (R, w2_scales), (2 * R, wb_scales)):
-            width = scales.shape[2]
-            nc.sync.dma_start(raw_scales[0:16, c0 : c0 + width].bitcast(I32), scales[0].bitcast(I32))
+        nc.sync.dma_start(xf_sb[1][:], xf_rows[:, 1, :])
+        xf_pair = pool.tile([P, 2, T], F32, name="xf_pair")
+        nc.sync.dma_start(xf_pair[:], xf_rows[:, 2:4, :])
         fk_sb = pool.tile([P, PACK], F32, name="fk_sb")
         nc.sync.dma_start(fk_sb[:], fk.rearrange("(p t) o -> p (t o)", t=PACK))
-        so_sb = pool.tile([P, PACK, J], F32, name="so_sb")
-        nc.sync.dma_start(so_sb[:], so.rearrange("(p t) j -> p t j", t=PACK))
+        so_rest = pool.tile([P, PACK * J - LEAD], F32, name="so_rest")
+        nc.sync.dma_start(so_rest[:], so_rows[:, LEAD:])
         fl_sb = pool.tile([P, PACK], F32, name="fl_sb")
         nc.sync.dma_start(fl_sb[:], fl.rearrange("(p t) o -> p (t o)", t=PACK))
-        nc.sync.dma_start(xf_sb[1][:], xf_rows[:, 2:4, :])
-        raw_words = []
-        for g, words in enumerate((w_words, w2_words)):
-            raw = pool.tile([P, 2 * R], U8, name=f"raw_words{g}")
-            nc.sync.dma_start(raw[:].bitcast(I32), words[0].bitcast(I32))
-            raw_words.append(raw)
+        raw_words = [pool.tile([P, 2 * R], U8, name=f"raw_words{g}", tag=f"raw_words{g}") for g in range(2)]
+        nc.sync.dma_start(raw_words[0][:].bitcast(I32), w_words[0].bitcast(I32))
+        xo_rows = xo.rearrange("(p t) c -> p t c", t=PACK)
+        xo_sb = [pool.tile([P, Z], F32, name=f"xo_sb{t}") for t in range(PACK)]
+        nc.sync.dma_start(xo_sb[0][:], xo_rows[:, 0, :])
         offs2_sb = pool.tile([P, J // 16], U16, name="offs2_sb")
         nc.sync.dma_start(offs2_sb[:], offs2)
-        xo_rows = xo.rearrange("(p t) c -> p t c", t=PACK)
-        xo_sb = []
-        for t in range(PACK):
-            plane = pool.tile([P, Z], F32, name=f"xo_sb{t}")
-            nc.sync.dma_start(plane[:], xo_rows[:, t, :])
-            xo_sb.append(plane)
+        for t in range(1, PACK):
+            nc.sync.dma_start(xo_sb[t][:], xo_rows[:, t, :])
+        nc.sync.dma_start(raw_words[1][:].bitcast(I32), w2_words[0].bitcast(I32))
         wb_sb = pool.tile([P, 2 * N], U8, name="wb_sb", align_bytes=64)
         nc.sync.dma_start(wb_sb[:].bitcast(I32), wb_words[0].bitcast(I32))
+        wb_sc = pool.tile([P, N], U8, name="wb_sc", align_bytes=64)
+        nc.vector.memset(wb_sc[:].bitcast(I32), 0)
+        for q in range(4):
+            nc.sync.dma_start(
+                wb_sc[32 * q : 32 * q + 4, :].bitcast(I32), wb_scales[0, 4 * q : 4 * q + 4, :].bitcast(I32)
+            )
+        rs_sb = pool.tile([P, 2, J], F32, name="rs_sb")
+        nc.sync.dma_start(rs_sb[:], rs.rearrange("(h p) j -> p h j", p=P))
         gm_sb = pool.tile([P, 2, 1], F32, name="gm_sb")
         with nc.allow_non_contiguous_dma(reason="one factor a partition and output tile"):
             nc.sync.dma_start(gm_sb[:], gm.rearrange("(h p) o -> p h o", p=P))
-        rs_sb = pool.tile([P, 2, J], F32, name="rs_sb")
-        nc.sync.dma_start(rs_sb[:], rs.rearrange("(h p) j -> p h j", p=P))
 
 
-        w_sc = pool.tile([P, 2 * R + N], U8, name="w_sc", align_bytes=64)
+        w_sc = pool.tile([P, 2 * R], U8, name="w_sc", align_bytes=64)
         nc.vector.tensor_copy(
-            w_sc[:, 0 : 2 * R].rearrange("p (g t m) -> p g t m", g=2, t=PACK),
-            raw_scales[:, 0 : 2 * R].rearrange("p (g m t) -> p g t m", g=2, t=PACK),
+            w_sc[:].rearrange("p (g t m) -> p g t m", g=2, t=PACK),
+            raw_scales[:].rearrange("p (g m t) -> p g t m", g=2, t=PACK),
         )
-        nc.vector.tensor_copy(w_sc[:, 2 * R :].bitcast(I32), raw_scales[:, 2 * R :].bitcast(I32))
         for q in range(1, 4):
             nc.gpsimd.dma_start(w_sc[32 * q : 32 * q + 4, :].bitcast(I32), w_sc[4 * q : 4 * q + 4, :].bitcast(I32))
 
@@ -87,87 +94,95 @@ def tile_list_sum_steps_gated_lagged_residual_kernel(
         ha = pool.tile([P, (2 + J) * PACK], F32, name="ha")
         nc.vector.memset(ha[:, 0 : 2 * PACK], 0.0)
 
+        sig = pool.tile([P, PACK * J], F32, name="sig")
+        gate = [pool.tile([P, 2, J], F32, name=f"gate{u}", tag=f"gate{u}", align_bytes=64) for u in range(2)]
+        nc.scalar.activation(sig[:, 0:LEAD], so_first[:], ACT.Sigmoid)
         steps = pool.tile([P, PACK, J], F32, name="steps")
-        u = pool.tile([P, PACK, J], F32, name="u")
         for t in range(2):
-            nc.vector.tensor_copy(picked[0][:, t, PAD:], xf_sb[0][:, t, :].indirect(offs_sb[:]))
+            nc.vector.tensor_copy(picked[0][:, t, PAD:], xf_sb[t][:].indirect(offs_sb[:]))
         nc.vector.scalar_tensor_tensor(
             steps[:, 0:2, :], picked[0][:, :, PAD - 1 : PAD - 1 + J], -0.6, picked[0][:, :, PAD:], ALU.mult, ALU.add
         )
-        for t in range(2):
-            nc.vector.tensor_scalar(u[:, t, :], steps[:, t, :], fk_sb[:, t : t + 1], None, ALU.mult)
-        sig = pool.tile([P, PACK, J], F32, name="sig")
-        nc.scalar.activation(sig[:], so_sb[:], ACT.Sigmoid)
-        nc.vector.tensor_copy(picked[1][:, 0, PAD:], xf_sb[1][:, 0, :].indirect(offs_sb[:]))
-        nc.scalar.activation(picked[1][:, 1, PAD:], xf_sb[1][:, 1, :].indirect(offs_sb[:]), ACT.Copy)
+        nc.scalar.activation(picked[1][:, 0, PAD:], xf_pair[:, 0, :].indirect(offs_sb[:]), ACT.Copy)
+        nc.vector.tensor_copy(picked[1][:, 1, PAD:], xf_pair[:, 1, :].indirect(offs_sb[:]))
         nc.vector.scalar_tensor_tensor(
             steps[:, 2:4, :], picked[1][:, :, PAD - 1 : PAD - 1 + J], -0.6, picked[1][:, :, PAD:], ALU.mult, ALU.add
         )
-        gate = pool.tile([P, PACK, J], F32, name="gate")
-        for t in range(PACK):
-            nc.scalar.activation(gate[:, t, :], sig[:, t, :], ACT.Copy, scale=fl_sb[:, t : t + 1])
-        w_sb = []
-        for g in range(2):
-            dealt = pool.tile([P, 2 * R], U8, name=f"w_sb{g}", align_bytes=64)
-            nc.vector.tensor_copy(
-                dealt[:].bitcast(U16).rearrange("p (t m) -> p t m", t=PACK),
+        nc.scalar.activation(sig[:, LEAD : 2 * J], so_rest[:, 0 : 2 * J - LEAD], ACT.Sigmoid)
+        for t in range(2):
+            nc.scalar.activation(gate[t // 2][:, t % 2, :], sig[:, t * J : (t + 1) * J], ACT.Copy, scale=fl_sb[:, t : t + 1])
+        nc.scalar.activation(sig[:, 2 * J :], so_rest[:, 2 * J - LEAD :], ACT.Sigmoid)
+        for t in range(2, PACK):
+            nc.scalar.activation(gate[t // 2][:, t % 2, :], sig[:, t * J : (t + 1) * J], ACT.Copy, scale=fl_sb[:, t : t + 1])
+        w_sb = [pool.tile([P, 2 * R], U8, name=f"w_sb{g}", align_bytes=64) for g in range(2)]
+
+        def deal_words(g, copy):
+            copy(
+                w_sb[g][:].bitcast(U16).rearrange("p (t m) -> p t m", t=PACK),
                 raw_words[g][:].bitcast(U16).rearrange("p (m t) -> p t m", t=PACK),
             )
-            w_sb.append(dealt)
-        for t in range(2, PACK):
-            nc.scalar.activation(u[:, t, :], steps[:, t, :], ACT.Copy, scale=fk_sb[:, t : t + 1])
-        u_bf = pool.tile([P, J * PACK], BF16, name="u_bf", align_bytes=64)
+
+        deal_words(0, nc.scalar.copy)
+        u_bf = [pool.tile([P, HALF * PACK], BF16, name=f"u_bf{s}", align_bytes=64) for s in range(2)]
+        u_sc = [pool.tile([P, HALF], U8, name=f"u_sc{s}", align_bytes=64) for s in range(2)]
+        nc.vector.tensor_tensor(
+            u_bf[0][:].rearrange("p (c i t) -> p c t i", i=4, t=PACK),
+            steps[:, :, 0:HALF].rearrange("p t (c i) -> p c t i", i=4),
+            fk_sb[:].rearrange("p (c t i) -> p c t i", c=1, i=1).to_broadcast([P, HALF // 4, PACK, 4]),
+            ALU.mult,
+        )
+        u_late = pool.tile([P, PACK, HALF], F32, name="u_late", tag="raw_words0")
+        for t in range(PACK):
+            nc.scalar.activation(u_late[:, t, :], steps[:, t, HALF:], ACT.Copy, scale=fk_sb[:, t : t + 1])
         nc.scalar.copy(
-            u_bf[:].rearrange("p (c i t) -> p c t i", i=4, t=PACK), u[:].rearrange("p t (c i) -> p c t i", i=4)
+            u_bf[1][:].rearrange("p (c i t) -> p c t i", i=4, t=PACK), u_late[:].rearrange("p t (c i) -> p c t i", i=4)
         )
 
-        u2 = pool.tile([P, PACK, J], F32, name="u2")
-        for t in range(2):
-            nc.vector.tensor_tensor(u2[:, t, :], xo_sb[t][:].indirect(offs2_sb[:]), gate[:, t, :], ALU.mult)
-
-        u_codes = pool.tile([P, J], U32, name="u_codes", align_bytes=64)
-        u_sc = pool.tile([P, J], U8, name="u_sc", align_bytes=64)
-        nc.vector.quantize_mx(out=u_codes[:].bitcast(E4M3), scales=u_sc[:], in_=u_bf[:])
         acc = [psum.tile([P, PACK, HALF], F32, name=f"acc{s}") for s in range(2)]
-        for s in range(2):
-            cols = slice(s * HALF, (s + 1) * HALF)
+
+        def first_product(s, tag):
+            u_codes = pool.tile([P, HALF], U32, name=f"u_codes{s}", tag=tag, align_bytes=64)
+            nc.vector.quantize_mx(out=u_codes[:].bitcast(E4M3), scales=u_sc[s][:], in_=u_bf[s][:])
             for t in range(PACK):
                 nc.tensor.matmul_mx(
                     acc[s][:, t, :],
                     lhsT=w_sb[0][:, 2 * P * t : 2 * P * (t + 1)].bitcast(E2M1),
                     lhsT_scale=w_sc[:, P * t : P * (t + 1)],
-                    rhs=u_codes[:, cols].bitcast(E4M3),
-                    rhs_scale=u_sc[:, cols],
+                    rhs=u_codes[:].bitcast(E4M3),
+                    rhs_scale=u_sc[s][:],
                     start=(t == 0),
                     stop=False,
                 )
 
-        nc.vector.tensor_tensor(u2[:, 2, :], xo_sb[2][:].indirect(offs2_sb[:]), gate[:, 2, :], ALU.mult)
+        entries = [pool.tile([P, 2, J], F32, name=f"entries{u}") for u in range(2)]
+        u2_bf = pool.tile([P, J, PACK], BF16, name="u2_bf", align_bytes=64)
 
-        u2_bf = [pool.tile([P, HALF * PACK], BF16, name=f"u2_bf{s}", align_bytes=64) for s in range(2)]
+        def gate_and_weave(u, cols):
+            nc.vector.tensor_tensor(
+                u2_bf[:, cols, 2 * u : 2 * u + 2].rearrange("p (c i) t -> p c t i", i=4),
+                entries[u][:, :, cols].rearrange("p t (c i) -> p c t i", i=4),
+                gate[u][:, :, cols].rearrange("p t (c i) -> p c t i", i=4),
+                ALU.mult,
+            )
+
+        nc.vector.tensor_copy(entries[0][:, 0, :], xo_sb[0][:].indirect(offs2_sb[:]))
+        first_product(0, "u_codes0")
+        nc.vector.tensor_copy(entries[0][:, 1, :], xo_sb[1][:].indirect(offs2_sb[:]))
+        gate_and_weave(0, slice(0, J))
+        first_product(1, "gate0")
+        nc.vector.tensor_copy(entries[1][:, 0, :], xo_sb[2][:].indirect(offs2_sb[:]))
+
         u2_codes = [pool.tile([P, HALF], U32, name=f"u2_codes{s}", align_bytes=64) for s in range(2)]
         u2_sc = [pool.tile([P, HALF], U8, name=f"u2_sc{s}", align_bytes=64) for s in range(2)]
         hid_bf = [pool.tile([P, HALF * PACK], BF16, name=f"hid_bf{s}", align_bytes=64) for s in range(2)]
         hid_codes = [pool.tile([P, HALF], U32, name=f"hid_codes{s}", align_bytes=64) for s in range(2)]
         hid_sc = [pool.tile([P, HALF], U8, name=f"hid_sc{s}", align_bytes=64) for s in range(2)]
-        prod = [psum.tile([P, 2, HALF], F32, name=f"prod{s}") for s in range(2)]
+        prod = [[psum.tile([P, HALF], F32, name=f"prod{s}{h}") for h in range(2)] for s in range(2)]
         res = [pool.tile([P, 2, HALF], F32, name=f"res{s}") for s in range(2)]
         out_rows = out.rearrange("(h p) j -> p h j", p=P)
 
-        def gather_last(s):
-            cols = slice(s * HALF, (s + 1) * HALF)
-            lst = offs2_sb[:, s * HALF // 16 : (s + 1) * HALF // 16]
-            nc.vector.tensor_tensor(u2[:, 3, cols], xo_sb[3][:].indirect(lst), gate[:, 3, cols], ALU.mult)
-
-        def weave(s, copy):
-            cols = slice(s * HALF, (s + 1) * HALF)
-            copy(
-                u2_bf[s][:].rearrange("p (c i t) -> p c t i", i=4, t=PACK),
-                u2[:, :, cols].rearrange("p t (c i) -> p c t i", i=4),
-            )
-
         def first_stage(s):
-            nc.vector.quantize_mx(out=u2_codes[s][:].bitcast(E5M2), scales=u2_sc[s][:], in_=u2_bf[s][:])
+            nc.vector.quantize_mx(out=u2_codes[s][:].bitcast(E5M2), scales=u2_sc[s][:], in_=u2_bf[:, s * HALF : (s + 1) * HALF, :].rearrange("p j t -> p (j t)"))
             for t in range(PACK):
                 nc.tensor.matmul_mx(
                     acc[s][:, t, :],
@@ -204,9 +219,9 @@ def tile_list_sum_steps_gated_lagged_residual_kernel(
             nc.vector.quantize_mx(out=hid_codes[s][:].bitcast(E5M2), scales=hid_sc[s][:], in_=hid_bf[s][:])
             for h in range(2):
                 nc.tensor.matmul_mx(
-                    prod[s][:, h, :],
+                    prod[s][h][:],
                     lhsT=wb_sb[:, 2 * P * h : 2 * P * (h + 1)].bitcast(E2M1),
-                    lhsT_scale=w_sc[:, 2 * R + P * h : 2 * R + P * (h + 1)],
+                    lhsT_scale=wb_sc[:, P * h : P * (h + 1)],
                     rhs=hid_codes[s][:].bitcast(E5M2),
                     rhs_scale=hid_sc[s][:],
                     start=True,
@@ -217,14 +232,18 @@ def tile_list_sum_steps_gated_lagged_residual_kernel(
             cols = slice(s * HALF, (s + 1) * HALF)
             for h in range(2):
                 nc.vector.scalar_tensor_tensor(
-                    res[s][:, h, :], prod[s][:, h, :], gm_sb[:, h, :], rs_sb[:, h, cols], ALU.mult, ALU.add
+                    res[s][:, h, :], prod[s][h][:], gm_sb[:, h, :], rs_sb[:, h, cols], ALU.mult, ALU.add
                 )
-            nc.sync.dma_start(out_rows[:, :, cols], res[s][:])
+                if s == 1:
+                    nc.sync.dma_start(out_rows[:, h, cols], res[s][:, h, :])
+            if s == 0:
+                nc.sync.dma_start(out_rows[:, :, cols], res[s][:])
 
-        gather_last(0)
-        gather_last(1)
-        weave(0, nc.vector.tensor_copy)
-        weave(1, nc.scalar.copy)
+        nc.vector.tensor_copy(entries[1][:, 1, 0:HALF], xo_sb[3][:].indirect(offs2_sb[:, 0 : HALF // 16]))
+        nc.scalar.activation(entries[1][:, 1, HALF:], xo_sb[3][:].indirect(offs2_sb[:, HALF // 16 :]), ACT.Copy)
+        deal_words(1, nc.scalar.copy)
+        gate_and_weave(1, slice(0, HALF))
+        gate_and_weave(1, slice(HALF, J))
         first_stage(0)
         first_stage(1)
         hidden(0)

@@ -34,39 +34,49 @@ def tile_list_sum_steps_gated_lagged_residual_kernel(
 
         raw_scales = pool.tile([P, 2 * R], U8, name="raw_scales")
         nc.gpsimd.memset(raw_scales[:].bitcast(I32), 0)
-        for g, scales in enumerate((w_scales, w2_scales)):
-            nc.sync.dma_start(raw_scales[0:16, g * R : (g + 1) * R].bitcast(I32), scales[0].bitcast(I32))
-        so_rows = so.rearrange("(p t) j -> p (t j)", t=PACK)
-        so_first = pool.tile([P, LEAD], F32, name="so_first")
-        nc.sync.dma_start(so_first[:], so_rows[:, 0:LEAD])
         xf_rows = xf.rearrange("(p t) c -> p t c", t=PACK)
         xf_sb = [pool.tile([P, T], F32, name=f"xf_sb{t}") for t in range(2)]
         nc.sync.dma_start(xf_sb[0][:], xf_rows[:, 0, :])
         offs_sb = pool.tile([P, J // 16], U16, name="offs_sb")
         nc.sync.dma_start(offs_sb[:], offs)
+        so_rows = so.rearrange("(p t) j -> p (t j)", t=PACK)
+        so_first = pool.tile([P, LEAD], F32, name="so_first")
+        nc.sync.dma_start(so_first[:], so_rows[:, 0:LEAD])
         nc.sync.dma_start(xf_sb[1][:], xf_rows[:, 1, :])
+        for g, scales in enumerate((w_scales, w2_scales)):
+            nc.sync.dma_start(raw_scales[0:16, g * R : (g + 1) * R].bitcast(I32), scales[0].bitcast(I32))
         xf_pair = pool.tile([P, 2, T], F32, name="xf_pair")
         nc.sync.dma_start(xf_pair[:], xf_rows[:, 2:4, :])
+        fl_sb = pool.tile([P, PACK], F32, name="fl_sb")
+        nc.sync.dma_start(fl_sb[:], fl.rearrange("(p t) o -> p (t o)", t=PACK))
         fk_sb = pool.tile([P, PACK], F32, name="fk_sb")
         nc.sync.dma_start(fk_sb[:], fk.rearrange("(p t) o -> p (t o)", t=PACK))
         so_rest = pool.tile([P, PACK * J - LEAD], F32, name="so_rest")
         nc.sync.dma_start(so_rest[:], so_rows[:, LEAD:])
-        fl_sb = pool.tile([P, PACK], F32, name="fl_sb")
-        nc.sync.dma_start(fl_sb[:], fl.rearrange("(p t) o -> p (t o)", t=PACK))
-        raw_words = [pool.tile([P, 2 * R], U8, name=f"raw_words{g}", tag=f"raw_words{g}") for g in range(2)]
-        nc.sync.dma_start(raw_words[0][:].bitcast(I32), w_words[0].bitcast(I32))
         xo_rows = xo.rearrange("(p t) c -> p t c", t=PACK)
         xo_sb = [pool.tile([P, Z], F32, name=f"xo_sb{t}") for t in range(PACK)]
         nc.sync.dma_start(xo_sb[0][:], xo_rows[:, 0, :])
+        raw_words = [pool.tile([P, 2 * R], U8, name=f"raw_words{g}", tag=f"raw_words{g}") for g in range(2)]
+        nc.sync.dma_start(raw_words[0][:].bitcast(I32), w_words[0].bitcast(I32))
         offs2_sb = pool.tile([P, J // 16], U16, name="offs2_sb")
         nc.sync.dma_start(offs2_sb[:], offs2)
-        for t in range(1, PACK):
+        nc.sync.dma_start(xo_sb[1][:], xo_rows[:, 1, :])
+
+        w_sc = pool.tile([P, 2 * R], U8, name="w_sc", align_bytes=64)
+        nc.vector.tensor_copy(
+            w_sc[:].rearrange("p (g t m) -> p g t m", g=2, t=PACK),
+            raw_scales[:].rearrange("p (g m t) -> p g t m", g=2, t=PACK),
+        )
+        for q in range(1, 4):
+            nc.sync.dma_start(w_sc[32 * q : 32 * q + 4, :].bitcast(I32), w_sc[4 * q : 4 * q + 4, :].bitcast(I32))
+
+        for t in range(2, PACK):
             nc.sync.dma_start(xo_sb[t][:], xo_rows[:, t, :])
         nc.sync.dma_start(raw_words[1][:].bitcast(I32), w2_words[0].bitcast(I32))
         wb_sb = pool.tile([P, 2 * N], U8, name="wb_sb", align_bytes=64)
         nc.sync.dma_start(wb_sb[:].bitcast(I32), wb_words[0].bitcast(I32))
         wb_sc = pool.tile([P, N], U8, name="wb_sc", align_bytes=64)
-        nc.vector.memset(wb_sc[:].bitcast(I32), 0)
+        nc.gpsimd.memset(wb_sc[:].bitcast(I32), 0)
         for q in range(4):
             nc.sync.dma_start(
                 wb_sc[32 * q : 32 * q + 4, :].bitcast(I32), wb_scales[0, 4 * q : 4 * q + 4, :].bitcast(I32)
@@ -77,15 +87,6 @@ def tile_list_sum_steps_gated_lagged_residual_kernel(
         with nc.allow_non_contiguous_dma(reason="one factor a partition and output tile"):
             nc.sync.dma_start(gm_sb[:], gm.rearrange("(h p) o -> p h o", p=P))
 
-
-        w_sc = pool.tile([P, 2 * R], U8, name="w_sc", align_bytes=64)
-        nc.vector.tensor_copy(
-            w_sc[:].rearrange("p (g t m) -> p g t m", g=2, t=PACK),
-            raw_scales[:].rearrange("p (g m t) -> p g t m", g=2, t=PACK),
-        )
-        for q in range(1, 4):
-            nc.gpsimd.dma_start(w_sc[32 * q : 32 * q + 4, :].bitcast(I32), w_sc[4 * q : 4 * q + 4, :].bitcast(I32))
-
         picked = []
         for u in range(2):
             pair = pool.tile([P, 2, PAD + J], F32, name=f"picked{u}")
@@ -95,25 +96,30 @@ def tile_list_sum_steps_gated_lagged_residual_kernel(
         nc.vector.memset(ha[:, 0 : 2 * PACK], 0.0)
 
         sig = pool.tile([P, PACK * J], F32, name="sig")
-        gate = [pool.tile([P, 2, J], F32, name=f"gate{u}", tag=f"gate{u}", align_bytes=64) for u in range(2)]
+        gate = [pool.tile([P, J], F32, name=f"gate{t}", tag=f"gate{t}", align_bytes=64) for t in range(PACK)]
         nc.scalar.activation(sig[:, 0:LEAD], so_first[:], ACT.Sigmoid)
         steps = pool.tile([P, PACK, J], F32, name="steps")
-        for t in range(2):
-            nc.vector.tensor_copy(picked[0][:, t, PAD:], xf_sb[t][:].indirect(offs_sb[:]))
-        nc.vector.scalar_tensor_tensor(
-            steps[:, 0:2, :], picked[0][:, :, PAD - 1 : PAD - 1 + J], -0.6, picked[0][:, :, PAD:], ALU.mult, ALU.add
-        )
+
+        def take_steps(t0, t1):
+            src = picked[t0 // 2][:, t0 % 2 : t0 % 2 + t1 - t0, :]
+            nc.vector.scalar_tensor_tensor(
+                steps[:, t0:t1, :], src[:, :, PAD - 1 : PAD - 1 + J], -0.6, src[:, :, PAD:], ALU.mult, ALU.add
+            )
+
+        nc.vector.tensor_copy(picked[0][:, 0, PAD:], xf_sb[0][:].indirect(offs_sb[:]))
+        nc.scalar.activation(picked[0][:, 1, PAD:], xf_sb[1][:].indirect(offs_sb[:]), ACT.Copy)
+        take_steps(0, 1)
+        take_steps(1, 2)
         nc.scalar.activation(picked[1][:, 0, PAD:], xf_pair[:, 0, :].indirect(offs_sb[:]), ACT.Copy)
         nc.vector.tensor_copy(picked[1][:, 1, PAD:], xf_pair[:, 1, :].indirect(offs_sb[:]))
-        nc.vector.scalar_tensor_tensor(
-            steps[:, 2:4, :], picked[1][:, :, PAD - 1 : PAD - 1 + J], -0.6, picked[1][:, :, PAD:], ALU.mult, ALU.add
-        )
+        take_steps(2, 3)
+        take_steps(3, 4)
         nc.scalar.activation(sig[:, LEAD : 2 * J], so_rest[:, 0 : 2 * J - LEAD], ACT.Sigmoid)
         for t in range(2):
-            nc.scalar.activation(gate[t // 2][:, t % 2, :], sig[:, t * J : (t + 1) * J], ACT.Copy, scale=fl_sb[:, t : t + 1])
+            nc.scalar.activation(gate[t][:], sig[:, t * J : (t + 1) * J], ACT.Copy, scale=fl_sb[:, t : t + 1])
         nc.scalar.activation(sig[:, 2 * J :], so_rest[:, 2 * J - LEAD :], ACT.Sigmoid)
         for t in range(2, PACK):
-            nc.scalar.activation(gate[t // 2][:, t % 2, :], sig[:, t * J : (t + 1) * J], ACT.Copy, scale=fl_sb[:, t : t + 1])
+            nc.scalar.activation(gate[t][:], sig[:, t * J : (t + 1) * J], ACT.Copy, scale=fl_sb[:, t : t + 1])
         w_sb = [pool.tile([P, 2 * R], U8, name=f"w_sb{g}", align_bytes=64) for g in range(2)]
 
         def deal_words(g, copy):
@@ -123,54 +129,52 @@ def tile_list_sum_steps_gated_lagged_residual_kernel(
             )
 
         deal_words(0, nc.scalar.copy)
-        u_bf = [pool.tile([P, HALF * PACK], BF16, name=f"u_bf{s}", align_bytes=64) for s in range(2)]
-        u_sc = [pool.tile([P, HALF], U8, name=f"u_sc{s}", align_bytes=64) for s in range(2)]
+        u_bf = pool.tile([P, J * PACK], BF16, name="u_bf", align_bytes=64)
         nc.vector.tensor_tensor(
-            u_bf[0][:].rearrange("p (c i t) -> p c t i", i=4, t=PACK),
-            steps[:, :, 0:HALF].rearrange("p t (c i) -> p c t i", i=4),
-            fk_sb[:].rearrange("p (c t i) -> p c t i", c=1, i=1).to_broadcast([P, HALF // 4, PACK, 4]),
+            u_bf[:].rearrange("p (c i t) -> p c t i", i=4, t=PACK),
+            steps[:].rearrange("p t (c i) -> p c t i", i=4),
+            fk_sb[:].rearrange("p (c t i) -> p c t i", c=1, i=1).to_broadcast([P, J // 4, PACK, 4]),
             ALU.mult,
         )
-        u_late = pool.tile([P, PACK, HALF], F32, name="u_late", tag="raw_words0")
-        for t in range(PACK):
-            nc.scalar.activation(u_late[:, t, :], steps[:, t, HALF:], ACT.Copy, scale=fk_sb[:, t : t + 1])
-        nc.scalar.copy(
-            u_bf[1][:].rearrange("p (c i t) -> p c t i", i=4, t=PACK), u_late[:].rearrange("p t (c i) -> p c t i", i=4)
-        )
-
         acc = [psum.tile([P, PACK, HALF], F32, name=f"acc{s}") for s in range(2)]
 
-        def first_product(s, tag):
-            u_codes = pool.tile([P, HALF], U32, name=f"u_codes{s}", tag=tag, align_bytes=64)
-            nc.vector.quantize_mx(out=u_codes[:].bitcast(E4M3), scales=u_sc[s][:], in_=u_bf[s][:])
-            for t in range(PACK):
-                nc.tensor.matmul_mx(
-                    acc[s][:, t, :],
-                    lhsT=w_sb[0][:, 2 * P * t : 2 * P * (t + 1)].bitcast(E2M1),
-                    lhsT_scale=w_sc[:, P * t : P * (t + 1)],
-                    rhs=u_codes[:].bitcast(E4M3),
-                    rhs_scale=u_sc[s][:],
-                    start=(t == 0),
-                    stop=False,
-                )
+        def first_product():
+            u_codes = pool.tile([P, J], U32, name="u_codes", tag="gate0", align_bytes=64)
+            u_sc = pool.tile([P, J], U8, name="u_sc", align_bytes=64)
+            nc.vector.quantize_mx(out=u_codes[:].bitcast(E4M3), scales=u_sc[:], in_=u_bf[:])
+            for s in range(2):
+                cols = slice(s * HALF, (s + 1) * HALF)
+                for t in range(PACK):
+                    nc.tensor.matmul_mx(
+                        acc[s][:, t, :],
+                        lhsT=w_sb[0][:, 2 * P * t : 2 * P * (t + 1)].bitcast(E2M1),
+                        lhsT_scale=w_sc[:, P * t : P * (t + 1)],
+                        rhs=u_codes[:, cols].bitcast(E4M3),
+                        rhs_scale=u_sc[:, cols],
+                        start=(t == 0),
+                        stop=False,
+                    )
 
-        entries = [pool.tile([P, 2, J], F32, name=f"entries{u}") for u in range(2)]
+        u2 = [pool.tile([P, 2, J], F32, name=f"u2_pair{u}") for u in range(2)]
         u2_bf = pool.tile([P, J, PACK], BF16, name="u2_bf", align_bytes=64)
 
-        def gate_and_weave(u, cols):
-            nc.vector.tensor_tensor(
+        def gather_gated(t, s0, s1):
+            cols = slice(s0 * HALF, s1 * HALF)
+            lst = offs2_sb[:, s0 * HALF // 16 : s1 * HALF // 16]
+            nc.vector.tensor_tensor(u2[t // 2][:, t % 2, cols], xo_sb[t][:].indirect(lst), gate[t][:, cols], ALU.mult)
+
+        def weave(u, s0, s1, copy):
+            cols = slice(s0 * HALF, s1 * HALF)
+            copy(
                 u2_bf[:, cols, 2 * u : 2 * u + 2].rearrange("p (c i) t -> p c t i", i=4),
-                entries[u][:, :, cols].rearrange("p t (c i) -> p c t i", i=4),
-                gate[u][:, :, cols].rearrange("p t (c i) -> p c t i", i=4),
-                ALU.mult,
+                u2[u][:, :, cols].rearrange("p t (c i) -> p c t i", i=4),
             )
 
-        nc.vector.tensor_copy(entries[0][:, 0, :], xo_sb[0][:].indirect(offs2_sb[:]))
-        first_product(0, "u_codes0")
-        nc.vector.tensor_copy(entries[0][:, 1, :], xo_sb[1][:].indirect(offs2_sb[:]))
-        gate_and_weave(0, slice(0, J))
-        first_product(1, "gate0")
-        nc.vector.tensor_copy(entries[1][:, 0, :], xo_sb[2][:].indirect(offs2_sb[:]))
+        gather_gated(0, 0, 2)
+        first_product()
+        gather_gated(1, 0, 2)
+        weave(0, 0, 2, nc.scalar.copy)
+        gather_gated(2, 0, 2)
 
         u2_codes = [pool.tile([P, HALF], U32, name=f"u2_codes{s}", align_bytes=64) for s in range(2)]
         u2_sc = [pool.tile([P, HALF], U8, name=f"u2_sc{s}", align_bytes=64) for s in range(2)]
@@ -239,16 +243,16 @@ def tile_list_sum_steps_gated_lagged_residual_kernel(
             if s == 0:
                 nc.sync.dma_start(out_rows[:, :, cols], res[s][:])
 
-        nc.vector.tensor_copy(entries[1][:, 1, 0:HALF], xo_sb[3][:].indirect(offs2_sb[:, 0 : HALF // 16]))
-        nc.scalar.activation(entries[1][:, 1, HALF:], xo_sb[3][:].indirect(offs2_sb[:, HALF // 16 :]), ACT.Copy)
         deal_words(1, nc.scalar.copy)
-        gate_and_weave(1, slice(0, HALF))
-        gate_and_weave(1, slice(HALF, J))
+        gather_gated(3, 0, 1)
+        gather_gated(3, 1, 2)
+        weave(1, 0, 1, nc.vector.tensor_copy)
+        weave(1, 1, 2, nc.vector.tensor_copy)
         first_stage(0)
         first_stage(1)
         hidden(0)
         second_stage(0)
         hidden(1)
-        finish(0)
         second_stage(1)
+        finish(0)
         finish(1)

@@ -35,7 +35,7 @@ def tile_list_sum_steps_gated_lagged_residual_kernel(
         raw_scales = pool.tile([P, 2 * R], U8, name="raw_scales")
         nc.gpsimd.memset(raw_scales[:].bitcast(I32), 0)
         xf_rows = xf.rearrange("(p t) c -> p t c", t=PACK)
-        xf_sb = [pool.tile([P, T], F32, name=f"xf_sb{t}") for t in range(2)]
+        xf_sb = [pool.tile([P, T], F32, name=f"xf_sb{t}") for t in range(PACK)]
         nc.sync.dma_start(xf_sb[0][:], xf_rows[:, 0, :])
         offs_sb = pool.tile([P, J // 16], U16, name="offs_sb")
         nc.sync.dma_start(offs_sb[:], offs)
@@ -45,8 +45,8 @@ def tile_list_sum_steps_gated_lagged_residual_kernel(
         nc.sync.dma_start(xf_sb[1][:], xf_rows[:, 1, :])
         for g, scales in enumerate((w_scales, w2_scales)):
             nc.sync.dma_start(raw_scales[0:16, g * R : (g + 1) * R].bitcast(I32), scales[0].bitcast(I32))
-        xf_pair = pool.tile([P, 2, T], F32, name="xf_pair")
-        nc.sync.dma_start(xf_pair[:], xf_rows[:, 2:4, :])
+        for t in range(2, PACK):
+            nc.sync.dma_start(xf_sb[t][:], xf_rows[:, t, :])
         fl_sb = pool.tile([P, PACK], F32, name="fl_sb")
         nc.sync.dma_start(fl_sb[:], fl.rearrange("(p t) o -> p (t o)", t=PACK))
         fk_sb = pool.tile([P, PACK], F32, name="fk_sb")
@@ -64,8 +64,8 @@ def tile_list_sum_steps_gated_lagged_residual_kernel(
 
         w_sc = pool.tile([P, 2 * R], U8, name="w_sc", align_bytes=64)
         nc.vector.tensor_copy(
-            w_sc[:].rearrange("p (g t m) -> p g t m", g=2, t=PACK),
-            raw_scales[:].rearrange("p (g m t) -> p g t m", g=2, t=PACK),
+            w_sc[:].rearrange("p (g t c i) -> p g c t i", g=2, t=PACK, i=16),
+            raw_scales[:].rearrange("p (g c i t) -> p g c t i", g=2, t=PACK, i=16),
         )
         for q in range(1, 4):
             nc.sync.dma_start(w_sc[32 * q : 32 * q + 4, :].bitcast(I32), w_sc[4 * q : 4 * q + 4, :].bitcast(I32))
@@ -109,11 +109,10 @@ def tile_list_sum_steps_gated_lagged_residual_kernel(
         nc.vector.tensor_copy(picked[0][:, 0, PAD:], xf_sb[0][:].indirect(offs_sb[:]))
         nc.scalar.activation(picked[0][:, 1, PAD:], xf_sb[1][:].indirect(offs_sb[:]), ACT.Copy)
         take_steps(0, 1)
-        take_steps(1, 2)
-        nc.scalar.activation(picked[1][:, 0, PAD:], xf_pair[:, 0, :].indirect(offs_sb[:]), ACT.Copy)
-        nc.vector.tensor_copy(picked[1][:, 1, PAD:], xf_pair[:, 1, :].indirect(offs_sb[:]))
-        take_steps(2, 3)
-        take_steps(3, 4)
+        nc.vector.tensor_copy(picked[1][:, 0, PAD:], xf_sb[2][:].indirect(offs_sb[:]))
+        nc.scalar.activation(picked[1][:, 1, PAD:], xf_sb[3][:].indirect(offs_sb[:]), ACT.Copy)
+        for t in range(1, PACK):
+            take_steps(t, t + 1)
         nc.scalar.activation(sig[:, LEAD : 2 * J], so_rest[:, 0 : 2 * J - LEAD], ACT.Sigmoid)
         for t in range(2):
             nc.scalar.activation(gate[t][:], sig[:, t * J : (t + 1) * J], ACT.Copy, scale=fl_sb[:, t : t + 1])
@@ -124,8 +123,8 @@ def tile_list_sum_steps_gated_lagged_residual_kernel(
 
         def deal_words(g, copy):
             copy(
-                w_sb[g][:].bitcast(U16).rearrange("p (t m) -> p t m", t=PACK),
-                raw_words[g][:].bitcast(U16).rearrange("p (m t) -> p t m", t=PACK),
+                w_sb[g][:].bitcast(U16).rearrange("p (t c i) -> p c t i", t=PACK, i=8),
+                raw_words[g][:].bitcast(U16).rearrange("p (c i t) -> p c t i", t=PACK, i=8),
             )
 
         deal_words(0, nc.scalar.copy)
@@ -139,7 +138,7 @@ def tile_list_sum_steps_gated_lagged_residual_kernel(
         acc = [psum.tile([P, PACK, HALF], F32, name=f"acc{s}") for s in range(2)]
 
         def first_product():
-            u_codes = pool.tile([P, J], U32, name="u_codes", tag="gate0", align_bytes=64)
+            u_codes = pool.tile([P, J], U32, name="u_codes", tag="gate1", align_bytes=64)
             u_sc = pool.tile([P, J], U8, name="u_sc", align_bytes=64)
             nc.vector.quantize_mx(out=u_codes[:].bitcast(E4M3), scales=u_sc[:], in_=u_bf[:])
             for s in range(2):
@@ -171,8 +170,8 @@ def tile_list_sum_steps_gated_lagged_residual_kernel(
             )
 
         gather_gated(0, 0, 2)
-        first_product()
         gather_gated(1, 0, 2)
+        first_product()
         weave(0, 0, 2, nc.scalar.copy)
         gather_gated(2, 0, 2)
 

from contextlib import ExitStack

import concourse.mybir as mybir

K, T, J, R, F, Z, N = 512, 512, 256, 512, 512, 1024, 256
FLOPS = 2 * J * (K * R + F * R + R * N)

F32 = mybir.dt.float32
BF16 = mybir.dt.bfloat16
I32 = mybir.dt.int32
U32 = mybir.dt.uint32
U16 = mybir.dt.uint16
U8 = mybir.dt.uint8
E4M3 = mybir.dt.float8_e4m3fn_x4
E5M2 = mybir.dt.float8_e5m2_x4
E2M1 = mybir.dt.float4_e2m1fn_x4
ALU = mybir.AluOpType
ACT = mybir.ActivationFunctionType

P = 128
PACK = 4
HALF = J // 2
PAD = 4
LEAD = 64


def tile_list_sum_steps_gated_lagged_residual_kernel(
    tc, xf, fk, w_words, w_scales, xo, fl, so, w2_words, w2_scales, wb_words, wb_scales, rs, gm, offs, offs2, out
):
    nc = tc.nc
    with ExitStack() as ctx:
        pool = ctx.enter_context(tc.tile_pool(name="keep", bufs=1))
        psum = ctx.enter_context(tc.psum_pool(name="psum", bufs=1))

        raw_scales = pool.tile([P, 2 * R], U8, name="raw_scales")
        nc.gpsimd.memset(raw_scales[:].bitcast(I32), 0)
        xf_rows = xf.rearrange("(p t) c -> p t c", t=PACK)
        xf_sb = [pool.tile([P, T], F32, name=f"xf_sb{t}") for t in range(PACK)]
        nc.sync.dma_start(xf_sb[0][:], xf_rows[:, 0, :])
        offs_sb = pool.tile([P, J // 16], U16, name="offs_sb")
        nc.sync.dma_start(offs_sb[:], offs)
        so_rows = so.rearrange("(p t) j -> p (t j)", t=PACK)
        so_first = pool.tile([P, LEAD], F32, name="so_first")
        nc.sync.dma_start(so_first[:], so_rows[:, 0:LEAD])
        nc.sync.dma_start(xf_sb[1][:], xf_rows[:, 1, :])
        for g, scales in enumerate((w_scales, w2_scales)):
            nc.sync.dma_start(raw_scales[0:16, g * R : (g + 1) * R].bitcast(I32), scales[0].bitcast(I32))
        for t in range(2, PACK):
            nc.sync.dma_start(xf_sb[t][:], xf_rows[:, t, :])
        fl_sb = pool.tile([P, PACK], F32, name="fl_sb")
        nc.sync.dma_start(fl_sb[:], fl.rearrange("(p t) o -> p (t o)", t=PACK))
        fk_sb = pool.tile([P, PACK], F32, name="fk_sb")
        nc.sync.dma_start(fk_sb[:], fk.rearrange("(p t) o -> p (t o)", t=PACK))
        so_rest = pool.tile([P, PACK * J - LEAD], F32, name="so_rest")
        nc.sync.dma_start(so_rest[:], so_rows[:, LEAD:])
        xo_rows = xo.rearrange("(p t) c -> p t c", t=PACK)
        xo_sb = [pool.tile([P, Z], F32, name=f"xo_sb{t}") for t in range(PACK)]
        nc.sync.dma_start(xo_sb[0][:], xo_rows[:, 0, :])
        raw_words = [pool.tile([P, 2 * R], U8, name=f"raw_words{g}", tag=f"raw_words{g}") for g in range(2)]
        nc.sync.dma_start(raw_words[0][:].bitcast(I32), w_words[0].bitcast(I32))
        offs2_sb = pool.tile([P, J // 16], U16, name="offs2_sb")
        nc.sync.dma_start(offs2_sb[:], offs2)
        nc.sync.dma_start(xo_sb[1][:], xo_rows[:, 1, :])

        w_sc = pool.tile([P, 2 * R], U8, name="w_sc", align_bytes=64)
        nc.vector.tensor_copy(
            w_sc[:].rearrange("p (g t c i) -> p g c t i", g=2, t=PACK, i=16),
            raw_scales[:].rearrange("p (g c i t) -> p g c t i", g=2, t=PACK, i=16),
        )
        for q in range(1, 4):
            nc.sync.dma_start(w_sc[32 * q : 32 * q + 4, :].bitcast(I32), w_sc[4 * q : 4 * q + 4, :].bitcast(I32))

        for t in range(2, PACK):
            nc.sync.dma_start(xo_sb[t][:], xo_rows[:, t, :])
        nc.sync.dma_start(raw_words[1][:].bitcast(I32), w2_words[0].bitcast(I32))
        wb_sb = pool.tile([P, 2 * N], U8, name="wb_sb", align_bytes=64)
        nc.sync.dma_start(wb_sb[:].bitcast(I32), wb_words[0].bitcast(I32))
        wb_sc = pool.tile([P, N], U8, name="wb_sc", align_bytes=64)
        nc.gpsimd.memset(wb_sc[:].bitcast(I32), 0)
        for q in range(4):
            nc.sync.dma_start(
                wb_sc[32 * q : 32 * q + 4, :].bitcast(I32), wb_scales[0, 4 * q : 4 * q + 4, :].bitcast(I32)
            )
        rs_sb = pool.tile([P, 2, J], F32, name="rs_sb")
        nc.sync.dma_start(rs_sb[:], rs.rearrange("(h p) j -> p h j", p=P))
        gm_sb = pool.tile([P, 2, 1], F32, name="gm_sb")
        with nc.allow_non_contiguous_dma(reason="one factor a partition and output tile"):
            nc.sync.dma_start(gm_sb[:], gm.rearrange("(h p) o -> p h o", p=P))

        picked = []
        for u in range(2):
            pair = pool.tile([P, 2, PAD + J], F32, name=f"picked{u}")
            nc.vector.memset(pair[:, :, PAD - 1 : PAD], 0.0)
            picked.append(pair)
        ha = pool.tile([P, (2 + J) * PACK], F32, name="ha")
        nc.vector.memset(ha[:, 0 : 2 * PACK], 0.0)

        sig = pool.tile([P, PACK * J], F32, name="sig")
        gate = [pool.tile([P, J], F32, name=f"gate{t}", tag=f"gate{t}", align_bytes=64) for t in range(PACK)]
        nc.scalar.activation(sig[:, 0:LEAD], so_first[:], ACT.Sigmoid)
        steps = pool.tile([P, PACK, J], F32, name="steps")

        def take_steps(t0, t1):
            src = picked[t0 // 2][:, t0 % 2 : t0 % 2 + t1 - t0, :]
            nc.vector.scalar_tensor_tensor(
                steps[:, t0:t1, :], src[:, :, PAD - 1 : PAD - 1 + J], -0.6, src[:, :, PAD:], ALU.mult, ALU.add
            )

        nc.vector.tensor_copy(picked[0][:, 0, PAD:], xf_sb[0][:].indirect(offs_sb[:]))
        nc.scalar.activation(picked[0][:, 1, PAD:], xf_sb[1][:].indirect(offs_sb[:]), ACT.Copy)
        take_steps(0, 1)
        nc.vector.tensor_copy(picked[1][:, 0, PAD:], xf_sb[2][:].indirect(offs_sb[:]))
        nc.scalar.activation(picked[1][:, 1, PAD:], xf_sb[3][:].indirect(offs_sb[:]), ACT.Copy)
        for t in range(1, PACK):
            take_steps(t, t + 1)
        nc.scalar.activation(sig[:, LEAD : 2 * J], so_rest[:, 0 : 2 * J - LEAD], ACT.Sigmoid)
        for t in range(2):
            nc.scalar.activation(gate[t][:], sig[:, t * J : (t + 1) * J], ACT.Copy, scale=fl_sb[:, t : t + 1])
        nc.scalar.activation(sig[:, 2 * J :], so_rest[:, 2 * J - LEAD :], ACT.Sigmoid)
        for t in range(2, PACK):
            nc.scalar.activation(gate[t][:], sig[:, t * J : (t + 1) * J], ACT.Copy, scale=fl_sb[:, t : t + 1])
        w_sb = [pool.tile([P, 2 * R], U8, name=f"w_sb{g}", align_bytes=64) for g in range(2)]

        def deal_words(g, copy):
            copy(
                w_sb[g][:].bitcast(U16).rearrange("p (t c i) -> p c t i", t=PACK, i=8),
                raw_words[g][:].bitcast(U16).rearrange("p (c i t) -> p c t i", t=PACK, i=8),
            )

        deal_words(0, nc.scalar.copy)
        u_bf = pool.tile([P, J * PACK], BF16, name="u_bf", align_bytes=64)
        nc.vector.tensor_tensor(
            u_bf[:].rearrange("p (c i t) -> p c t i", i=4, t=PACK),
            steps[:].rearrange("p t (c i) -> p c t i", i=4),
            fk_sb[:].rearrange("p (c t i) -> p c t i", c=1, i=1).to_broadcast([P, J // 4, PACK, 4]),
            ALU.mult,
        )
        acc = [psum.tile([P, PACK, HALF], F32, name=f"acc{s}") for s in range(2)]

        def first_product():
            u_codes = pool.tile([P, J], U32, name="u_codes", tag="gate1", align_bytes=64)
            u_sc = pool.tile([P, J], U8, name="u_sc", align_bytes=64)
            nc.vector.quantize_mx(out=u_codes[:].bitcast(E4M3), scales=u_sc[:], in_=u_bf[:])
            for s in range(2):
                cols = slice(s * HALF, (s + 1) * HALF)
                for t in range(PACK):
                    nc.tensor.matmul_mx(
                        acc[s][:, t, :],
                        lhsT=w_sb[0][:, 2 * P * t : 2 * P * (t + 1)].bitcast(E2M1),
                        lhsT_scale=w_sc[:, P * t : P * (t + 1)],
                        rhs=u_codes[:, cols].bitcast(E4M3),
                        rhs_scale=u_sc[:, cols],
                        start=(t == 0),
                        stop=False,
                    )

        u2 = [pool.tile([P, 2, J], F32, name=f"u2_pair{u}") for u in range(2)]
        u2_bf = pool.tile([P, J, PACK], BF16, name="u2_bf", align_bytes=64)

        def gather_gated(t, s0, s1):
            cols = slice(s0 * HALF, s1 * HALF)
            lst = offs2_sb[:, s0 * HALF // 16 : s1 * HALF // 16]
            nc.vector.tensor_tensor(u2[t // 2][:, t % 2, cols], xo_sb[t][:].indirect(lst), gate[t][:, cols], ALU.mult)

        def weave(u, s0, s1, copy):
            cols = slice(s0 * HALF, s1 * HALF)
            copy(
                u2_bf[:, cols, 2 * u : 2 * u + 2].rearrange("p (c i) t -> p c t i", i=4),
                u2[u][:, :, cols].rearrange("p t (c i) -> p c t i", i=4),
            )

        gather_gated(0, 0, 2)
        gather_gated(1, 0, 2)
        first_product()
        weave(0, 0, 2, nc.scalar.copy)
        gather_gated(2, 0, 2)

        u2_codes = [pool.tile([P, HALF], U32, name=f"u2_codes{s}", align_bytes=64) for s in range(2)]
        u2_sc = [pool.tile([P, HALF], U8, name=f"u2_sc{s}", align_bytes=64) for s in range(2)]
        hid_bf = [pool.tile([P, HALF * PACK], BF16, name=f"hid_bf{s}", align_bytes=64) for s in range(2)]
        hid_codes = [pool.tile([P, HALF], U32, name=f"hid_codes{s}", align_bytes=64) for s in range(2)]
        hid_sc = [pool.tile([P, HALF], U8, name=f"hid_sc{s}", align_bytes=64) for s in range(2)]
        prod = [[psum.tile([P, HALF], F32, name=f"prod{s}{h}") for h in range(2)] for s in range(2)]
        res = [pool.tile([P, 2, HALF], F32, name=f"res{s}") for s in range(2)]
        out_rows = out.rearrange("(h p) j -> p h j", p=P)

        def first_stage(s):
            nc.vector.quantize_mx(out=u2_codes[s][:].bitcast(E5M2), scales=u2_sc[s][:], in_=u2_bf[:, s * HALF : (s + 1) * HALF, :].rearrange("p j t -> p (j t)"))
            for t in range(PACK):
                nc.tensor.matmul_mx(
                    acc[s][:, t, :],
                    lhsT=w_sb[1][:, 2 * P * t : 2 * P * (t + 1)].bitcast(E2M1),
                    lhsT_scale=w_sc[:, R + P * t : R + P * (t + 1)],
                    rhs=u2_codes[s][:].bitcast(E5M2),
                    rhs_scale=u2_sc[s][:],
                    start=False,
                    stop=(t == PACK - 1),
                )

        QW = HALF // 2

        def hidden(s):
            for q in range(2):
                j0 = s * HALF + q * QW
                nc.scalar.activation(
                    ha[:, (2 + j0) * PACK : (2 + j0 + QW) * PACK].rearrange("p (j t) -> p j t", t=PACK),
                    acc[s][:, :, q * QW : (q + 1) * QW].rearrange("p t j -> p j t"),
                    ACT.Relu,
                )
            for q in range(2):
                j0 = s * HALF + q * QW
                nc.vector.scalar_tensor_tensor(
                    hid_bf[s][:, q * QW * PACK : (q + 1) * QW * PACK],
                    ha[:, j0 * PACK : (j0 + QW) * PACK],
                    -0.5,
                    ha[:, (2 + j0) * PACK : (2 + j0 + QW) * PACK],
                    ALU.mult,
                    ALU.add,
                )

        def second_stage(s):
            nc.vector.quantize_mx(out=hid_codes[s][:].bitcast(E5M2), scales=hid_sc[s][:], in_=hid_bf[s][:])
            for h in range(2):
                nc.tensor.matmul_mx(
                    prod[s][h][:],
                    lhsT=wb_sb[:, 2 * P * h : 2 * P * (h + 1)].bitcast(E2M1),
                    lhsT_scale=wb_sc[:, P * h : P * (h + 1)],
                    rhs=hid_codes[s][:].bitcast(E5M2),
                    rhs_scale=hid_sc[s][:],
                    start=True,
                    stop=True,
                )

        def finish(s):
            cols = slice(s * HALF, (s + 1) * HALF)
            for h in range(2):
                nc.vector.scalar_tensor_tensor(
                    res[s][:, h, :], prod[s][h][:], gm_sb[:, h, :], rs_sb[:, h, cols], ALU.mult, ALU.add
                )
                if s == 1:
                    nc.sync.dma_start(out_rows[:, h, cols], res[s][:, h, :])
            if s == 0:
                nc.sync.dma_start(out_rows[:, :, cols], res[s][:])

        deal_words(1, nc.scalar.copy)
        gather_gated(3, 0, 1)
        gather_gated(3, 1, 2)
        weave(1, 0, 1, nc.vector.tensor_copy)
        weave(1, 1, 2, nc.vector.tensor_copy)
        first_stage(0)
        first_stage(1)
        hidden(0)
        second_stage(0)
        hidden(1)
        second_stage(1)
        finish(0)
        finish(1)
